import numpy as np
import ml_dtypes


def mxq(x, axis, fmt="e4m3"):
    dtype, down = {"e4m3": (ml_dtypes.float8_e4m3fn, 7), "e5m2": (ml_dtypes.float8_e5m2, 14)}[fmt]
    v = np.moveaxis(np.asarray(x, np.float32).astype(ml_dtypes.bfloat16).astype(np.float64), axis, -1)
    blocks = v.reshape(v.shape[:-1] + (-1, 32))
    amax = np.abs(blocks).max(-1, keepdims=True)
    byte = np.maximum(np.where(amax > 0, np.frexp(amax)[1] - 1 + 127, 0) - down, 1)
    scale = np.exp2(byte - 127.0)
    codes = (blocks / scale).astype(np.float32).astype(dtype).astype(np.float64)
    return np.moveaxis((codes * scale).reshape(v.shape), -1, axis)


WIDE = False


def mx_kscale(k):
    if not WIDE:
        return np.ones(k)
    levels = np.array([10, -10, 5, -5, 0])
    if k % 512:
        return np.exp2(np.random.permutation(np.resize(levels, k // 32))).repeat(32)
    a = np.empty((k // 512, 16))
    for p in range(k // 512):
        a[p, :8] = np.random.permutation(np.resize(levels, 8))
        for g in range(8):
            far = levels[np.abs(levels - a[p, g]) >= 10]
            a[p, g + 8] = far[np.random.randint(len(far))]
    return np.exp2(a.ravel()).repeat(32)


def f64(x):
    return np.asarray(x).astype(np.float64)


def striped(idx):
    return np.tile(np.asarray(idx).reshape(-1, 16).T, (8, 1)).astype(np.uint16)


def unstriped(offs):
    return offs[:16].T.reshape(-1).astype(np.int64)


E2M1 = np.array([0.0, 0.5, 1.0, 1.5, 2.0, 3.0, 4.0, 6.0, -0.0, -0.5, -1.0, -1.5, -2.0, -3.0, -4.0, -6.0])


def pack_weight(w, fmt):
    k, n = w.shape
    w = f64(np.asarray(w, np.float32).astype(ml_dtypes.bfloat16)).reshape(k // 32, 32, n)
    amax = np.abs(w).max(1)
    if fmt == "e4m3":
        byte = np.frexp(amax)[1] - 1 + 127 - 7
    else:
        mant, ex = np.frexp(amax / 6.0)
        byte = np.where(mant > 0.5, ex, ex - 1) + 127
    byte = np.clip(np.where(amax > 0, byte, 1), 1, 254)
    scaled = (w * np.exp2(127.0 - byte)[:, None, :]).reshape(k, n).astype(np.float32)
    by_word = np.ascontiguousarray(scaled.reshape(k // 512, 128, 4, n).transpose(0, 1, 3, 2))
    if fmt == "e4m3":
        words = by_word.astype(ml_dtypes.float8_e4m3fn).view(np.uint8)
    else:
        c = by_word.astype(ml_dtypes.float4_e2m1fn).view(np.uint8) & 0xF
        words = (c[..., 0::2] | (c[..., 1::2] << 4)).reshape(k // 512, 128, 2 * n)
    return np.ascontiguousarray(words), np.ascontiguousarray(byte.astype(np.uint8).reshape(k // 512, 16, n))


def unpack_weight(words, scales, fmt):
    g, _, n = scales.shape
    words = np.ascontiguousarray(words).reshape(g, 128, n, -1)
    if fmt == "e4m3":
        vals = words.view(ml_dtypes.float8_e4m3fn).astype(np.float64)
    else:
        nib = np.empty((g, 128, n, 4), np.uint8)
        nib[..., 0::2] = words & 0xF
        nib[..., 1::2] = words >> 4
        vals = E2M1[nib]
    vals = vals * np.repeat(np.exp2(scales.astype(np.float64) - 127.0), 8, axis=1)[..., None]
    return vals.transpose(0, 1, 3, 2).reshape(g * 512, n)


def softplus(v):
    return np.log(1.0 + np.exp(v))


def bf(x):
    return np.asarray(x, np.float32).astype(ml_dtypes.bfloat16)


def planes(Y):
    r, m = Y.shape
    b = f64(bf(Y)).reshape(r // 32, 32, m)
    amax = np.abs(b).max(1)
    byte = np.clip(np.where(amax > 0, np.frexp(amax)[1] - 1 + 127 - 7, 1), 1, 254)
    codes = (b * np.exp2(127.0 - byte)[:, None, :]).reshape(r, m).astype(np.float32).astype(ml_dtypes.float8_e4m3fn).view(np.uint8)
    words = codes.reshape(r // 512, 128, 4, m).transpose(0, 1, 3, 2)
    return np.ascontiguousarray(words), np.ascontiguousarray(byte.astype(np.uint8).reshape(r // 512, 16, m))


D, E, T, I, Q = 512, 512, 2048, 512, 256


def setup_inputs():
    n = np.random.standard_normal
    idx = np.random.permutation(T)[:I]
    fd = mx_kscale(D)
    fi = mx_kscale(I)
    ti = np.ones(T)
    ti[idx] = fi
    keysp = pack_weight(n((D, T)) / fd[:, None], "e2m1")
    return {
        "query": (n((D, Q)) * 0.6 / np.sqrt(D) * fd[:, None]).astype(np.float32),
        "query2": (n((D, Q)) * 1.0 / np.sqrt(D) * fd[:, None]).astype(np.float32),
        "keys_words": keysp[0],
        "keys_scales": keysp[1],
        "strict": (np.random.uniform(0.4, 1.2, (Q, 1))).astype(np.float32),
        "os": (np.random.uniform(4.0, 16.0, (1, I)) * fi).astype(np.float32),
        "vals": (n((E, T)) / ti).astype(np.float32),
        "offs": striped(idx),
    }


def reference(query, query2, keys_words, keys_scales, strict, os, vals, offs):
    idx = unstriped(offs)
    keysu = unpack_weight(keys_words, keys_scales, "e2m1")
    queryq = mxq(f64(query), 0, "e4m3")
    keysidxg = keysu[:, idx]
    a = queryq.T @ keysidxg
    query2q = mxq(f64(query2), 0, "e4m3")
    b = query2q.T @ keysidxg
    s = a - softplus(b) * f64(strict)
    p = np.exp(s - np.max(s, axis=1, keepdims=True))
    z = np.sum(p, axis=1, keepdims=True)
    w = p / z
    wo1 = w * f64(os)
    wt1 = wo1.T
    vt1 = f64(vals)[:, idx].T
    vt1q = mxq(vt1, 0, "e4m3")
    wt1q = mxq(wt1, 0, "e4m3")
    o = vt1q.T @ wt1q
    words, scales = planes(o)
    return o, words, scales

@@ -1,0 +1,209 @@
+from contextlib import ExitStack
+
+import concourse.mybir as mybir
+from concourse.masks import make_identity
+
+D, E, T, I, Q = 512, 512, 2048, 512, 256
+FLOPS = 2 * (2 * D * Q * I + I * E * Q)
+
+F32 = mybir.dt.float32
+BF16 = mybir.dt.bfloat16
+I32 = mybir.dt.int32
+U32 = mybir.dt.uint32
+U16 = mybir.dt.uint16
+U8 = mybir.dt.uint8
+FP8X4 = mybir.dt.float8_e4m3fn_x4
+FP4X4 = mybir.dt.float4_e2m1fn_x4
+ALU = mybir.AluOpType
+ACT = mybir.ActivationFunctionType
+AXIS = mybir.AxisListType
+
+P = 128
+PACK = 4
+QT = Q // P
+
+
+def tile_attend_heldback_pl_kernel(tc, query, query2, keys_words, keys_scales, strict, slot_factor, vals, offs, out_0, out_1, out_2):
+    nc = tc.nc
+    with ExitStack() as ctx:
+        sb = ctx.enter_context(tc.tile_pool(name="sb", bufs=1))
+        ps = ctx.enter_context(tc.psum_pool(name="ps", bufs=1))
+
+        offsets = sb.tile([P, I // 16], U16, name="offsets")
+        nc.sync.dma_start(offsets[:], offs)
+
+        key_pool = sb.tile([P, T], U16, name="key_pool", align_bytes=64)
+        scale_pool = sb.tile([P, T], U8, name="scale_pool", align_bytes=64)
+        nc.gpsimd.memset(scale_pool[:].bitcast(I32), 0)
+        nc.sync.dma_start(key_pool[:].bitcast(I32), keys_words[0].bitcast(I32))
+        for quad in range(4):
+            nc.sync.dma_start(
+                scale_pool[32 * quad : 32 * quad + 4, :].bitcast(I32),
+                keys_scales[0, 4 * quad : 4 * quad + 4, :].bitcast(I32),
+            )
+        q2_raw = sb.tile([P, PACK, Q], F32, name="q2_raw", align_bytes=64)
+        nc.sync.dma_start(q2_raw[:], query2.rearrange("(p t) q -> p t q", t=PACK))
+        val_rows = vals.rearrange("(p t) n -> t p n", t=PACK)
+        val_pool = [sb.tile([P, T], F32, name="val_pool%d" % t, align_bytes=64) for t in range(PACK)]
+        for t in (0, 1):
+            nc.sync.dma_start(val_pool[t][:], val_rows[t])
+        strict_sb = sb.tile([P, QT], F32, name="strict_sb")
+        with nc.allow_non_contiguous_dma(reason="one strictness a partition"):
+            nc.sync.dma_start(strict_sb[:], strict.rearrange("(m p) o -> p (m o)", p=P))
+        os_sb = sb.tile([P, PACK], F32, name="os_sb")
+        nc.sync.dma_start(os_sb[:], slot_factor.rearrange("o (p c) -> p (o c)", c=PACK))
+        q_raw = sb.tile([P, PACK, Q], F32, name="q_raw")
+        nc.sync.dma_start(q_raw[:], query.rearrange("(p t) q -> p t q", t=PACK))
+        for t in (2, 3):
+            nc.sync.dma_start(val_pool[t][:], val_rows[t])
+        ident = sb.tile([P, P], F32, name="ident")
+        make_identity(nc, ident[:])
+
+        key_g = sb.tile([P, I], U16, name="key_g", align_bytes=64)
+        scale_g = sb.tile([P, I], U8, name="scale_g", align_bytes=64)
+        nc.vector.tensor_copy(key_g[:], key_pool[:].indirect(offsets[:]))
+        nc.vector.tensor_copy(scale_g[:], scale_pool[:].indirect(offsets[:]))
+
+        def grouped_views(grouped, raw):
+            return (
+                grouped.rearrange("p (c i) t -> p c t i", i=4),
+                raw.rearrange("p t (c i) -> p c t i", i=4),
+            )
+
+        def quantize(name, grouped):
+            width = grouped.shape[1]
+            codes = sb.tile([P, width], U32, name=name + "_codes", align_bytes=64)
+            scales = sb.tile([P, width], U8, name=name + "_scales", align_bytes=64)
+            nc.vector.quantize_mx(codes[:].bitcast(FP8X4), scales[:], grouped.rearrange("p c t -> p (c t)"))
+            return codes, scales
+
+        def scores(bank, codes, scales):
+            nc.tensor.matmul_mx(bank, lhsT=codes.bitcast(FP8X4), lhsT_scale=scales,
+                                rhs=key_g[:].bitcast(FP4X4), rhs_scale=scale_g[:], start=True, stop=True)
+
+        b_ps = []
+        q2_g = sb.tile([P, Q, PACK], BF16, name="q2_g", align_bytes=64)
+        for m in range(QT):
+            cols = slice(m * P, (m + 1) * P)
+            nc.scalar.copy(*grouped_views(q2_g[:, cols, :], q2_raw[:, :, cols]))
+            codes, scales = quantize("q2_%d" % m, q2_g[:, cols, :])
+            bank = ps.tile([P, I], F32, name="b_ps%d" % m)
+            scores(bank[:], codes[:], scales[:])
+            b_ps.append(bank)
+
+        mag = [sb.tile([P, I], F32, name="mag%d" % m) for m in range(QT)]
+        decay = [sb.tile([P, I], F32, name="decay%d" % m, align_bytes=64) for m in range(QT)]
+        tail = [sb.tile([P, I], F32, name="tail%d" % m) for m in range(QT)]
+        for m in range(QT):
+            nc.scalar.activation(mag[m][:], b_ps[m][:], ACT.Abs)
+            nc.scalar.activation(decay[m][:], mag[m][:], ACT.Exp, scale=-1.0)
+        for m in range(QT):
+            nc.scalar.activation(tail[m][:], decay[m][:], ACT.Ln, bias=1.0)
+
+        def turn(bank, rows):
+            words = rows.bitcast(F32)
+            for u in range(2):
+                nc.tensor.transpose(bank[:, u, :], words[:, u : 2 * P : 2], ident[:])
+
+        def gather_values(t, after, bank_tag):
+            g = sb.tile([P, I], BF16, name="val_g%d" % t, tag=after, align_bytes=64)
+            nc.vector.tensor_copy(g[:], val_pool[t][:].indirect(offsets[:]))
+            bank = ps.tile([P, 2, P], F32, name="vt_ps%d" % t, tag=bank_tag)
+            turn(bank, g[:])
+            return bank
+
+        def interleave(grouped, bank):
+            nc.scalar.copy(grouped.bitcast(F32), bank[:].rearrange("p u c -> p c u"))
+
+        vt_ps0 = gather_values(0, "q2_raw", "vt0")
+        vt_ps1 = gather_values(1, "q2_g", "vt1")
+
+        os_ps = ps.tile([P, PACK, P], F32, name="os_ps")
+        for c in range(PACK):
+            nc.tensor.transpose(os_ps[:, c, :], os_sb[:, c : c + 1].to_broadcast([P, P]), ident[:])
+
+        q_g = sb.tile([P, Q, PACK], BF16, name="q_g", tag="val_pool0", align_bytes=64)
+        nc.vector.tensor_copy(*grouped_views(q_g[:], q_raw[:]))
+        q_codes, q_scales = quantize("q", q_g[:])
+        a_ps = []
+        for m in range(QT):
+            cols = slice(m * P, (m + 1) * P)
+            bank = ps.tile([P, I], F32, name="a_ps%d" % m)
+            scores(bank[:], q_codes[:, cols], q_scales[:, cols])
+            a_ps.append(bank)
+
+        soft = [sb.tile([P, I], F32, name="soft%d" % m, align_bytes=64) for m in range(QT)]
+        neg_s = [sb.tile([P, I], F32, name="neg_s%d" % m) for m in range(QT)]
+        low = [sb.tile([P, 1], F32, name="low%d" % m) for m in range(QT)]
+        for m in range(QT):
+            nc.vector.scalar_tensor_tensor(soft[m][:], b_ps[m][:], 0.0, tail[m][:], ALU.max, ALU.add)
+        for m in range(QT):
+            nc.vector.scalar_tensor_tensor(neg_s[m][:], soft[m][:], strict_sb[:, m : m + 1], a_ps[m][:], ALU.mult, ALU.subtract)
+        for m in range(QT):
+            nc.vector.tensor_reduce(low[m][:], neg_s[m][:], AXIS.X, ALU.min)
+
+        vt01 = sb.tile([P, 2 * P, PACK], BF16, name="vt01", tag="decay1", align_bytes=64)
+        interleave(vt01[:, 0:P, :], vt_ps0)
+        interleave(vt01[:, P : 2 * P, :], vt_ps1)
+
+        prob = [sb.tile([P, I], F32, name="prob%d" % m, align_bytes=64) for m in range(QT)]
+        z = [sb.tile([P, 1], F32, name="z%d" % m) for m in range(QT)]
+        for m in range(QT):
+            nc.scalar.activation(prob[m][:], neg_s[m][:], ACT.Exp, bias=low[m][:], scale=-1.0, accum_out=z[m][:])
+        codes01, scales01 = quantize("v01", vt01[:])
+        v_ops = [(codes01[:, t * P : (t + 1) * P], scales01[:, t * P : (t + 1) * P]) for t in range(2)]
+
+        def late_values(t, after, bank_tag):
+            bank = gather_values(t, after, bank_tag)
+            vt = sb.tile([P, P, PACK], BF16, name="vt%d" % t, align_bytes=64)
+            interleave(vt[:], bank)
+            codes, scales = quantize("v%d" % t, vt[:])
+            v_ops.append((codes[:], scales[:]))
+
+        wt_ps = ps.tile([P, QT, 2, P], F32, name="wt_ps")
+
+        def weights(m):
+            rz = sb.tile([P, 1], F32, name="rz%d" % m)
+            nc.vector.reciprocal(rz[:], z[m][:])
+            w = sb.tile([P, I], BF16, name="w%d" % m)
+            nc.vector.scalar_tensor_tensor(
+                w[:].rearrange("p (n c) -> p n c", c=PACK), prob[m][:].rearrange("p (n c) -> p n c", c=PACK),
+                rz[:], os_ps[:].rearrange("p c n -> p n c"), ALU.mult, ALU.mult)
+            turn(wt_ps[:, m], w[:])
+            wt = sb.tile([P, P, PACK], BF16, name="wt%d" % m, align_bytes=64)
+            interleave(wt[:], wt_ps[:, m])
+            return quantize("w%d" % m, wt[:])
+
+        y_codes = sb.tile([P, Q], U32, name="y_codes", align_bytes=64)
+        y_scales = sb.tile([P, Q], U8, name="y_scales", align_bytes=64)
+        out_rows = out_0.rearrange("(p t) q -> p t q", t=PACK)
+        out_words = out_1[0].rearrange("l c r -> l (c r)").bitcast(I32)
+
+        def result(m, w_op, bank_tags):
+            cols = slice(m * P, (m + 1) * P)
+            y = sb.tile([P, PACK, P], F32, name="y%d" % m)
+            for h in range(2):
+                bank = ps.tile([P, 2, P], F32, name="o_ps%d%d" % (m, h), tag=bank_tags[h])
+                for j in range(2):
+                    codes, scales = v_ops[2 * h + j]
+                    nc.tensor.matmul_mx(bank[:, j, :], lhsT=codes.bitcast(FP8X4), lhsT_scale=scales,
+                                        rhs=w_op[0][:].bitcast(FP8X4), rhs_scale=w_op[1][:], start=True, stop=True)
+                nc.scalar.copy(y[:, 2 * h : 2 * h + 2, :], bank[:])
+            nc.sync.dma_start(out_rows[:, :, cols], y[:])
+            yg = sb.tile([P, P, PACK], BF16, name="yg%d" % m, align_bytes=64)
+            nc.vector.tensor_copy(*grouped_views(yg[:], y[:]))
+            nc.vector.quantize_mx(y_codes[:, cols].bitcast(FP8X4), y_scales[:, cols], yg[:].rearrange("p q t -> p (q t)"))
+            nc.sync.dma_start(out_words[:, cols], y_codes[:, cols].bitcast(I32))
+
+        late_values(2, "soft1", "b_ps0")
+        w0 = weights(0)
+        late_values(3, "prob0", "b_ps1")
+        w1 = weights(1)
+        result(0, w0, ("a_ps0", "a_ps1"))
+        result(1, w1, ("vt0", "vt1"))
+        for quad in range(4):
+            queue = nc.sync if quad % 2 else nc.scalar
+            queue.dma_start(
+                out_2[0, 4 * quad : 4 * quad + 4, :].bitcast(I32),
+                y_scales[32 * quad : 32 * quad + 4, :].bitcast(I32),
+            )

@@ -32,6 +32,8 @@ def tile_attend_heldback_pl_kernel(tc, query, query2, keys_words, keys_scales, s
         offsets = sb.tile([P, I // 16], U16, name="offsets")
         nc.sync.dma_start(offsets[:], offs)
 
+        os_sb = sb.tile([P, PACK], F32, name="os_sb")
+        nc.sync.dma_start(os_sb[:], slot_factor.rearrange("o (p c) -> p (o c)", c=PACK))
         key_pool = sb.tile([P, T], U16, name="key_pool", align_bytes=64)
         scale_pool = sb.tile([P, T], U8, name="scale_pool", align_bytes=64)
         nc.gpsimd.memset(scale_pool[:].bitcast(I32), 0)
@@ -45,19 +47,24 @@ def tile_attend_heldback_pl_kernel(tc, query, query2, keys_words, keys_scales, s
         nc.sync.dma_start(q2_raw[:], query2.rearrange("(p t) q -> p t q", t=PACK))
         val_rows = vals.rearrange("(p t) n -> t p n", t=PACK)
         val_pool = [sb.tile([P, T], F32, name="val_pool%d" % t, align_bytes=64) for t in range(PACK)]
-        for t in (0, 1):
-            nc.sync.dma_start(val_pool[t][:], val_rows[t])
+        nc.sync.dma_start(val_pool[0][:], val_rows[0])
+        q_raw = sb.tile([P, PACK, Q], F32, name="q_raw")
+        nc.sync.dma_start(q_raw[:], query.rearrange("(p t) q -> p t q", t=PACK))
+        nc.sync.dma_start(val_pool[1][:], val_rows[1])
         strict_sb = sb.tile([P, QT], F32, name="strict_sb")
         with nc.allow_non_contiguous_dma(reason="one strictness a partition"):
             nc.sync.dma_start(strict_sb[:], strict.rearrange("(m p) o -> p (m o)", p=P))
-        os_sb = sb.tile([P, PACK], F32, name="os_sb")
-        nc.sync.dma_start(os_sb[:], slot_factor.rearrange("o (p c) -> p (o c)", c=PACK))
-        q_raw = sb.tile([P, PACK, Q], F32, name="q_raw")
-        nc.sync.dma_start(q_raw[:], query.rearrange("(p t) q -> p t q", t=PACK))
         for t in (2, 3):
             nc.sync.dma_start(val_pool[t][:], val_rows[t])
         ident = sb.tile([P, P], F32, name="ident")
         make_identity(nc, ident[:])
+
+        os_ps = ps.tile([P, PACK, P], F32, name="os_ps")
+        for c in range(PACK):
+            nc.tensor.transpose(os_ps[:, c, :], os_sb[:, c : c + 1].to_broadcast([P, P]), ident[:])
+
+        os_row = sb.tile([P, I], F32, name="os_row")
+        nc.scalar.copy(os_row[:].rearrange("p (n c) -> p n c", c=PACK), os_ps[:].rearrange("p c n -> p n c"))
 
         key_g = sb.tile([P, I], U16, name="key_g", align_bytes=64)
         scale_g = sb.tile([P, I], U8, name="scale_g", align_bytes=64)
@@ -93,7 +100,7 @@ def tile_attend_heldback_pl_kernel(tc, query, query2, keys_words, keys_scales, s
 
         mag = [sb.tile([P, I], F32, name="mag%d" % m) for m in range(QT)]
         decay = [sb.tile([P, I], F32, name="decay%d" % m, align_bytes=64) for m in range(QT)]
-        tail = [sb.tile([P, I], F32, name="tail%d" % m) for m in range(QT)]
+        tail = [sb.tile([P, I], F32, name="tail%d" % m, tag=("mag1", "tail1")[m]) for m in range(QT)]
         for m in range(QT):
             nc.scalar.activation(mag[m][:], b_ps[m][:], ACT.Abs)
             nc.scalar.activation(decay[m][:], mag[m][:], ACT.Exp, scale=-1.0)
@@ -112,19 +119,18 @@ def tile_attend_heldback_pl_kernel(tc, query, query2, keys_words, keys_scales, s
             turn(bank, g[:])
             return bank
 
-        def interleave(grouped, bank):
-            nc.scalar.copy(grouped.bitcast(F32), bank[:].rearrange("p u c -> p c u"))
+        def interleave(copy, grouped, bank):
+            copy(grouped.bitcast(F32), bank[:].rearrange("p u c -> p c u"))
 
         vt_ps0 = gather_values(0, "q2_raw", "vt0")
-        vt_ps1 = gather_values(1, "q2_g", "vt1")
-
-        os_ps = ps.tile([P, PACK, P], F32, name="os_ps")
-        for c in range(PACK):
-            nc.tensor.transpose(os_ps[:, c, :], os_sb[:, c : c + 1].to_broadcast([P, P]), ident[:])
 
         q_g = sb.tile([P, Q, PACK], BF16, name="q_g", tag="val_pool0", align_bytes=64)
         nc.vector.tensor_copy(*grouped_views(q_g[:], q_raw[:]))
+        vt0 = sb.tile([P, P, PACK], BF16, name="vt0", align_bytes=64)
+        interleave(nc.vector.tensor_copy, vt0[:], vt_ps0)
         q_codes, q_scales = quantize("q", q_g[:])
+        v_ops = [quantize("v0", vt0[:])]
+        vt_ps1 = gather_values(1, "val_pool0", "vt1")
         a_ps = []
         for m in range(QT):
             cols = slice(m * P, (m + 1) * P)
@@ -132,7 +138,7 @@ def tile_attend_heldback_pl_kernel(tc, query, query2, keys_words, keys_scales, s
             scores(bank[:], q_codes[:, cols], q_scales[:, cols])
             a_ps.append(bank)
 
-        soft = [sb.tile([P, I], F32, name="soft%d" % m, align_bytes=64) for m in range(QT)]
+        soft = [sb.tile([P, I], F32, name="soft%d" % m, tag=("val_pool1", "soft1")[m], align_bytes=64) for m in range(QT)]
         neg_s = [sb.tile([P, I], F32, name="neg_s%d" % m) for m in range(QT)]
         low = [sb.tile([P, 1], F32, name="low%d" % m) for m in range(QT)]
         for m in range(QT):
@@ -142,65 +148,66 @@ def tile_attend_heldback_pl_kernel(tc, query, query2, keys_words, keys_scales, s
         for m in range(QT):
             nc.vector.tensor_reduce(low[m][:], neg_s[m][:], AXIS.X, ALU.min)
 
-        vt01 = sb.tile([P, 2 * P, PACK], BF16, name="vt01", tag="decay1", align_bytes=64)
-        interleave(vt01[:, 0:P, :], vt_ps0)
-        interleave(vt01[:, P : 2 * P, :], vt_ps1)
+        vt1 = sb.tile([P, P, PACK], BF16, name="vt1", tag="decay1", align_bytes=64)
+        interleave(nc.scalar.copy, vt1[:], vt_ps1)
 
         prob = [sb.tile([P, I], F32, name="prob%d" % m, align_bytes=64) for m in range(QT)]
         z = [sb.tile([P, 1], F32, name="z%d" % m) for m in range(QT)]
         for m in range(QT):
             nc.scalar.activation(prob[m][:], neg_s[m][:], ACT.Exp, bias=low[m][:], scale=-1.0, accum_out=z[m][:])
-        codes01, scales01 = quantize("v01", vt01[:])
-        v_ops = [(codes01[:, t * P : (t + 1) * P], scales01[:, t * P : (t + 1) * P]) for t in range(2)]
+        v_ops.append(quantize("v1", vt1[:]))
 
         def late_values(t, after, bank_tag):
             bank = gather_values(t, after, bank_tag)
             vt = sb.tile([P, P, PACK], BF16, name="vt%d" % t, align_bytes=64)
-            interleave(vt[:], bank)
-            codes, scales = quantize("v%d" % t, vt[:])
-            v_ops.append((codes[:], scales[:]))
+            interleave(nc.scalar.copy, vt[:], bank)
+            v_ops.append(quantize("v%d" % t, vt[:]))
 
         wt_ps = ps.tile([P, QT, 2, P], F32, name="wt_ps")
+
+        wt = sb.tile([P, Q, PACK], BF16, name="wt", align_bytes=64)
 
         def weights(m):
             rz = sb.tile([P, 1], F32, name="rz%d" % m)
             nc.vector.reciprocal(rz[:], z[m][:])
             w = sb.tile([P, I], BF16, name="w%d" % m)
-            nc.vector.scalar_tensor_tensor(
-                w[:].rearrange("p (n c) -> p n c", c=PACK), prob[m][:].rearrange("p (n c) -> p n c", c=PACK),
-                rz[:], os_ps[:].rearrange("p c n -> p n c"), ALU.mult, ALU.mult)
-            turn(wt_ps[:, m], w[:])
-            wt = sb.tile([P, P, PACK], BF16, name="wt%d" % m, align_bytes=64)
-            interleave(wt[:], wt_ps[:, m])
-            return quantize("w%d" % m, wt[:])
-
-        y_codes = sb.tile([P, Q], U32, name="y_codes", align_bytes=64)
-        y_scales = sb.tile([P, Q], U8, name="y_scales", align_bytes=64)
-        out_rows = out_0.rearrange("(p t) q -> p t q", t=PACK)
-        out_words = out_1[0].rearrange("l c r -> l (c r)").bitcast(I32)
-
-        def result(m, w_op, bank_tags):
-            cols = slice(m * P, (m + 1) * P)
-            y = sb.tile([P, PACK, P], F32, name="y%d" % m)
-            for h in range(2):
-                bank = ps.tile([P, 2, P], F32, name="o_ps%d%d" % (m, h), tag=bank_tags[h])
-                for j in range(2):
-                    codes, scales = v_ops[2 * h + j]
-                    nc.tensor.matmul_mx(bank[:, j, :], lhsT=codes.bitcast(FP8X4), lhsT_scale=scales,
-                                        rhs=w_op[0][:].bitcast(FP8X4), rhs_scale=w_op[1][:], start=True, stop=True)
-                nc.scalar.copy(y[:, 2 * h : 2 * h + 2, :], bank[:])
-            nc.sync.dma_start(out_rows[:, :, cols], y[:])
-            yg = sb.tile([P, P, PACK], BF16, name="yg%d" % m, align_bytes=64)
-            nc.vector.tensor_copy(*grouped_views(yg[:], y[:]))
-            nc.vector.quantize_mx(y_codes[:, cols].bitcast(FP8X4), y_scales[:, cols], yg[:].rearrange("p q t -> p (q t)"))
-            nc.sync.dma_start(out_words[:, cols], y_codes[:, cols].bitcast(I32))
+            if m == 0:
+                nc.vector.scalar_tensor_tensor(
+                    w[:].rearrange("p (n c) -> p n c", c=PACK), prob[m][:].rearrange("p (n c) -> p n c", c=PACK),
+                    rz[:], os_ps[:].rearrange("p c n -> p n c"), ALU.mult, ALU.mult)
+                turn(wt_ps[:, m], w[:])
+            else:
+                po = sb.tile([P, I], F32, name="po")
+                nc.gpsimd.tensor_tensor(po[:], prob[m][:], os_row[:], ALU.mult)
+                nc.scalar.activation(w[:].rearrange("p (u c v) -> p u c v", u=2, v=2),
+                                     po[:].rearrange("p (c u v) -> p u c v", u=2, v=2), ACT.Copy, scale=rz[:])
+                words = w[:].bitcast(F32)
+                for u in range(2):
+                    nc.tensor.transpose(wt_ps[:, m, u, :], words[:, u * P : (u + 1) * P], ident[:])
+            interleave(nc.scalar.copy, wt[:, m * P : (m + 1) * P, :], wt_ps[:, m])
 
         late_values(2, "soft1", "b_ps0")
-        w0 = weights(0)
+        weights(0)
+        weights(1)
+        w_codes, w_scales = quantize("w", wt[:])
         late_values(3, "prob0", "b_ps1")
-        w1 = weights(1)
-        result(0, w0, ("a_ps0", "a_ps1"))
-        result(1, w1, ("vt0", "vt1"))
+
+        out_rows = out_0.rearrange("(p t) q -> p t q", t=PACK)
+        y = sb.tile([P, PACK, Q], F32, name="y")
+        for places, tag in ((range(0, 2), "a_ps0"), (range(2, 3), "a_ps1"), (range(3, 4), "vt0")):
+            bank = ps.tile([P, len(places), Q], F32, name="o_ps%d" % places.start, tag=tag)
+            for j, t in enumerate(places):
+                codes, scales = v_ops[t]
+                nc.tensor.matmul_mx(bank[:, j, :], lhsT=codes[:].bitcast(FP8X4), lhsT_scale=scales[:],
+                                    rhs=w_codes[:].bitcast(FP8X4), rhs_scale=w_scales[:], start=True, stop=True)
+            nc.scalar.copy(y[:, places.start : places.stop, :], bank[:])
+            if places.stop >= 3:
+                rows = slice(0, 3) if places.stop == 3 else slice(3, 4)
+                nc.sync.dma_start(out_rows[:, rows, :], y[:, rows, :])
+        yg = sb.tile([P, Q, PACK], BF16, name="yg", align_bytes=64)
+        nc.vector.tensor_copy(*grouped_views(yg[:], y[:]))
+        y_codes, y_scales = quantize("y", yg[:])
+        nc.sync.dma_start(out_1[0].rearrange("l c r -> l (c r)").bitcast(I32), y_codes[:].bitcast(I32))
         for quad in range(4):
             queue = nc.sync if quad % 2 else nc.scalar
             queue.dma_start(

@@ -38,11 +38,9 @@ def tile_attend_heldback_pl_kernel(tc, query, query2, keys_words, keys_scales, s
         scale_pool = sb.tile([P, T], U8, name="scale_pool", align_bytes=64)
         nc.gpsimd.memset(scale_pool[:].bitcast(I32), 0)
         nc.sync.dma_start(key_pool[:].bitcast(I32), keys_words[0].bitcast(I32))
-        for quad in range(4):
-            nc.sync.dma_start(
-                scale_pool[32 * quad : 32 * quad + 4, :].bitcast(I32),
-                keys_scales[0, 4 * quad : 4 * quad + 4, :].bitcast(I32),
-            )
+        scale_rows = keys_scales[0].bitcast(I32).rearrange("(g r) n -> r g n", r=4)
+        for r in range(4):
+            nc.sync.dma_start(scale_pool[:].bitcast(I32)[r:P:32, :], scale_rows[r])
         q2_raw = sb.tile([P, PACK, Q], F32, name="q2_raw", align_bytes=64)
         nc.sync.dma_start(q2_raw[:], query2.rearrange("(p t) q -> p t q", t=PACK))
         val_rows = vals.rearrange("(p t) n -> t p n", t=PACK)
@@ -77,9 +75,9 @@ def tile_attend_heldback_pl_kernel(tc, query, query2, keys_words, keys_scales, s
                 raw.rearrange("p t (c i) -> p c t i", i=4),
             )
 
-        def quantize(name, grouped):
+        def quantize(name, grouped, after=None):
             width = grouped.shape[1]
-            codes = sb.tile([P, width], U32, name=name + "_codes", align_bytes=64)
+            codes = sb.tile([P, width], U32, name=name + "_codes", tag=after or name + "_codes", align_bytes=64)
             scales = sb.tile([P, width], U8, name=name + "_scales", align_bytes=64)
             nc.vector.quantize_mx(codes[:].bitcast(FP8X4), scales[:], grouped.rearrange("p c t -> p (c t)"))
             return codes, scales
@@ -148,69 +146,70 @@ def tile_attend_heldback_pl_kernel(tc, query, query2, keys_words, keys_scales, s
         for m in range(QT):
             nc.vector.tensor_reduce(low[m][:], neg_s[m][:], AXIS.X, ALU.min)
 
-        vt1 = sb.tile([P, P, PACK], BF16, name="vt1", tag="decay1", align_bytes=64)
-        interleave(nc.scalar.copy, vt1[:], vt_ps1)
+        vt12 = sb.tile([P, 2 * P, PACK], BF16, name="vt12", tag="decay1", align_bytes=64)
+        interleave(nc.scalar.copy, vt12[:, 0:P, :], vt_ps1)
 
         prob = [sb.tile([P, I], F32, name="prob%d" % m, align_bytes=64) for m in range(QT)]
-        z = [sb.tile([P, 1], F32, name="z%d" % m) for m in range(QT)]
+        z = sb.tile([P, QT], F32, name="z")
         for m in range(QT):
-            nc.scalar.activation(prob[m][:], neg_s[m][:], ACT.Exp, bias=low[m][:], scale=-1.0, accum_out=z[m][:])
-        v_ops.append(quantize("v1", vt1[:]))
+            nc.scalar.activation(prob[m][:], neg_s[m][:], ACT.Exp, bias=low[m][:], scale=-1.0, accum_out=z[:, m : m + 1])
 
-        def late_values(t, after, bank_tag):
-            bank = gather_values(t, after, bank_tag)
-            vt = sb.tile([P, P, PACK], BF16, name="vt%d" % t, align_bytes=64)
-            interleave(nc.scalar.copy, vt[:], bank)
-            v_ops.append(quantize("v%d" % t, vt[:]))
-
-        wt_ps = ps.tile([P, QT, 2, P], F32, name="wt_ps")
-
+        vt_ps2 = gather_values(2, "soft1", "b_ps0")
+        rz = sb.tile([P, QT], F32, name="rz")
+        nc.vector.reciprocal(rz[:], z[:])
+        w = [sb.tile([P, I], BF16, name="w%d" % m) for m in range(QT)]
+        wt_ps = [ps.tile([P, 2, P], F32, name="wt_ps%d" % m, tag=("wt0", "vt1")[m]) for m in range(QT)]
+        po = sb.tile([P, I], F32, name="po", align_bytes=64)
+        nc.gpsimd.tensor_tensor(po[:], prob[0][:], os_row[:], ALU.mult)
+        nc.scalar.activation(w[0][:].rearrange("p (u c v) -> p u c v", u=2, v=2),
+                             po[:].rearrange("p (c u v) -> p u c v", u=2, v=2), ACT.Copy, scale=rz[:, 0:1])
+        for u in range(2):
+            nc.tensor.transpose(wt_ps[0][:, u, :], w[0][:].bitcast(F32)[:, u * P : (u + 1) * P], ident[:])
+        nc.vector.scalar_tensor_tensor(
+            w[1][:].rearrange("p (n c) -> p n c", c=PACK), prob[1][:].rearrange("p (n c) -> p n c", c=PACK),
+            rz[:, 1:2], os_ps[:].rearrange("p c n -> p n c"), ALU.mult, ALU.mult)
+        turn(wt_ps[1], w[1][:])
+        vt_ps3 = gather_values(3, "prob1", "b_ps1")
+        interleave(nc.scalar.copy, vt12[:, P : 2 * P, :], vt_ps2)
         wt = sb.tile([P, Q, PACK], BF16, name="wt", align_bytes=64)
+        for m in range(QT):
+            interleave(nc.scalar.copy, wt[:, m * P : (m + 1) * P, :], wt_ps[m])
+        w_codes, w_scales = quantize("w", wt[:], after="val_pool3")
+        codes12, scales12 = quantize("v12", vt12[:], after="wt")
+        vt3 = sb.tile([P, P, PACK], BF16, name="vt3", align_bytes=64)
+        interleave(nc.scalar.copy, vt3[:], vt_ps3)
+        codes3, scales3 = quantize("v3", vt3[:], after="decay1")
+        stationary = [(v_ops[0][0][:], v_ops[0][1][:]), (codes12[:, 0:P], scales12[:, 0:P]),
+                      (codes12[:, P : 2 * P], scales12[:, P : 2 * P]), (codes3[:], scales3[:])]
 
-        def weights(m):
-            rz = sb.tile([P, 1], F32, name="rz%d" % m)
-            nc.vector.reciprocal(rz[:], z[m][:])
-            w = sb.tile([P, I], BF16, name="w%d" % m)
-            if m == 0:
-                nc.vector.scalar_tensor_tensor(
-                    w[:].rearrange("p (n c) -> p n c", c=PACK), prob[m][:].rearrange("p (n c) -> p n c", c=PACK),
-                    rz[:], os_ps[:].rearrange("p c n -> p n c"), ALU.mult, ALU.mult)
-                turn(wt_ps[:, m], w[:])
-            else:
-                po = sb.tile([P, I], F32, name="po")
-                nc.gpsimd.tensor_tensor(po[:], prob[m][:], os_row[:], ALU.mult)
-                nc.scalar.activation(w[:].rearrange("p (u c v) -> p u c v", u=2, v=2),
-                                     po[:].rearrange("p (c u v) -> p u c v", u=2, v=2), ACT.Copy, scale=rz[:])
-                words = w[:].bitcast(F32)
-                for u in range(2):
-                    nc.tensor.transpose(wt_ps[:, m, u, :], words[:, u * P : (u + 1) * P], ident[:])
-            interleave(nc.scalar.copy, wt[:, m * P : (m + 1) * P, :], wt_ps[:, m])
-
-        late_values(2, "soft1", "b_ps0")
-        weights(0)
-        weights(1)
-        w_codes, w_scales = quantize("w", wt[:])
-        late_values(3, "prob0", "b_ps1")
+        def product(bank, t, cols):
+            nc.tensor.matmul_mx(bank, lhsT=stationary[t][0].bitcast(FP8X4), lhsT_scale=stationary[t][1],
+                                rhs=w_codes[:, cols].bitcast(FP8X4), rhs_scale=w_scales[:, cols], start=True, stop=True)
 
         out_rows = out_0.rearrange("(p t) q -> p t q", t=PACK)
+        out_words = out_1[0].rearrange("l c r -> l (c r)").bitcast(I32)
         y = sb.tile([P, PACK, Q], F32, name="y")
-        for places, tag in ((range(0, 2), "a_ps0"), (range(2, 3), "a_ps1"), (range(3, 4), "vt0")):
-            bank = ps.tile([P, len(places), Q], F32, name="o_ps%d" % places.start, tag=tag)
-            for j, t in enumerate(places):
-                codes, scales = v_ops[t]
-                nc.tensor.matmul_mx(bank[:, j, :], lhsT=codes[:].bitcast(FP8X4), lhsT_scale=scales[:],
-                                    rhs=w_codes[:].bitcast(FP8X4), rhs_scale=w_scales[:], start=True, stop=True)
-            nc.scalar.copy(y[:, places.start : places.stop, :], bank[:])
-            if places.stop >= 3:
-                rows = slice(0, 3) if places.stop == 3 else slice(3, 4)
-                nc.sync.dma_start(out_rows[:, rows, :], y[:, rows, :])
-        yg = sb.tile([P, Q, PACK], BF16, name="yg", align_bytes=64)
-        nc.vector.tensor_copy(*grouped_views(yg[:], y[:]))
-        y_codes, y_scales = quantize("y", yg[:])
-        nc.sync.dma_start(out_1[0].rearrange("l c r -> l (c r)").bitcast(I32), y_codes[:].bitcast(I32))
-        for quad in range(4):
-            queue = nc.sync if quad % 2 else nc.scalar
-            queue.dma_start(
-                out_2[0, 4 * quad : 4 * quad + 4, :].bitcast(I32),
-                y_scales[32 * quad : 32 * quad + 4, :].bitcast(I32),
-            )
+        for t, tag in enumerate(("a_ps0", "a_ps1", "vt0")):
+            bank = ps.tile([P, Q], F32, name="o_ps%d" % t, tag=tag)
+            product(bank[:], t, slice(0, Q))
+            nc.scalar.copy(y[:, t, :], bank[:])
+        nc.sync.dma_start(out_rows[:, 0:3, :], y[:, 0:3, :])
+        y_codes = sb.tile([P, Q], U32, name="y_codes", align_bytes=64)
+        y_scales = sb.tile([P, Q], U8, name="y_scales", align_bytes=64)
+        yg = []
+        for m, tag in enumerate(("wt0", "vt1")):
+            cols = slice(m * P, (m + 1) * P)
+            bank = ps.tile([P, P], F32, name="o_ps3%d" % m, tag=tag)
+            product(bank[:], 3, cols)
+            nc.scalar.copy(y[:, 3, cols], bank[:])
+            yg.append(sb.tile([P, P, PACK], BF16, name="yg%d" % m, align_bytes=64))
+            nc.vector.tensor_copy(*grouped_views(yg[m][:], y[:, :, cols]))
+        nc.sync.dma_start(out_rows[:, 3, :], y[:, 3, :])
+        for m in range(QT):
+            cols = slice(m * P, (m + 1) * P)
+            nc.vector.quantize_mx(y_codes[:, cols].bitcast(FP8X4), y_scales[:, cols], yg[m][:].rearrange("p q t -> p (q t)"))
+        nc.sync.dma_start(out_words, y_codes[:].bitcast(I32))
+        out_scales = out_2[0].bitcast(I32).rearrange("(g r) n -> r g n", r=4)
+        for r in range(4):
+            queue = nc.sync if r % 2 else nc.scalar
+            queue.dma_start(out_scales[r], y_scales[:].bitcast(I32)[r:P:32, :])

@@ -21,6 +21,8 @@ AXIS = mybir.AxisListType
 P = 128
 PACK = 4
 QT = Q // P
+QUADRANT = 32
+SCALE_ROWS = 4
 
 
 def tile_attend_heldback_pl_kernel(tc, query, query2, keys_words, keys_scales, strict, slot_factor, vals, offs, out_0, out_1, out_2):
@@ -34,13 +36,15 @@ def tile_attend_heldback_pl_kernel(tc, query, query2, keys_words, keys_scales, s
 
         os_sb = sb.tile([P, PACK], F32, name="os_sb")
         nc.sync.dma_start(os_sb[:], slot_factor.rearrange("o (p c) -> p (o c)", c=PACK))
+
         key_pool = sb.tile([P, T], U16, name="key_pool", align_bytes=64)
         scale_pool = sb.tile([P, T], U8, name="scale_pool", align_bytes=64)
         nc.gpsimd.memset(scale_pool[:].bitcast(I32), 0)
         nc.sync.dma_start(key_pool[:].bitcast(I32), keys_words[0].bitcast(I32))
-        scale_rows = keys_scales[0].bitcast(I32).rearrange("(g r) n -> r g n", r=4)
-        for r in range(4):
-            nc.sync.dma_start(scale_pool[:].bitcast(I32)[r:P:32, :], scale_rows[r])
+        scale_rows = keys_scales[0].bitcast(I32).rearrange("(g r) n -> r g n", r=SCALE_ROWS)
+        for r in range(SCALE_ROWS):
+            nc.sync.dma_start(scale_pool[:].bitcast(I32)[r:P:QUADRANT, :], scale_rows[r])
+
         q2_raw = sb.tile([P, PACK, Q], F32, name="q2_raw", align_bytes=64)
         nc.sync.dma_start(q2_raw[:], query2.rearrange("(p t) q -> p t q", t=PACK))
         val_rows = vals.rearrange("(p t) n -> t p n", t=PACK)
@@ -50,7 +54,7 @@ def tile_attend_heldback_pl_kernel(tc, query, query2, keys_words, keys_scales, s
         nc.sync.dma_start(q_raw[:], query.rearrange("(p t) q -> p t q", t=PACK))
         nc.sync.dma_start(val_pool[1][:], val_rows[1])
         strict_sb = sb.tile([P, QT], F32, name="strict_sb")
-        with nc.allow_non_contiguous_dma(reason="one strictness a partition"):
+        with nc.allow_non_contiguous_dma(reason="one strictness a partition and query tile"):
             nc.sync.dma_start(strict_sb[:], strict.rearrange("(m p) o -> p (m o)", p=P))
         for t in (2, 3):
             nc.sync.dma_start(val_pool[t][:], val_rows[t])
@@ -60,9 +64,6 @@ def tile_attend_heldback_pl_kernel(tc, query, query2, keys_words, keys_scales, s
         os_ps = ps.tile([P, PACK, P], F32, name="os_ps")
         for c in range(PACK):
             nc.tensor.transpose(os_ps[:, c, :], os_sb[:, c : c + 1].to_broadcast([P, P]), ident[:])
-
-        os_row = sb.tile([P, I], F32, name="os_row")
-        nc.scalar.copy(os_row[:].rearrange("p (n c) -> p n c", c=PACK), os_ps[:].rearrange("p c n -> p n c"))
 
         key_g = sb.tile([P, I], U16, name="key_g", align_bytes=64)
         scale_g = sb.tile([P, I], U8, name="scale_g", align_bytes=64)
@@ -137,7 +138,7 @@ def tile_attend_heldback_pl_kernel(tc, query, query2, keys_words, keys_scales, s
             a_ps.append(bank)
 
         soft = [sb.tile([P, I], F32, name="soft%d" % m, tag=("val_pool1", "soft1")[m], align_bytes=64) for m in range(QT)]
-        neg_s = [sb.tile([P, I], F32, name="neg_s%d" % m) for m in range(QT)]
+        neg_s = [sb.tile([P, I], F32, name="neg_s%d" % m, align_bytes=64) for m in range(QT)]
         low = [sb.tile([P, 1], F32, name="low%d" % m) for m in range(QT)]
         for m in range(QT):
             nc.vector.scalar_tensor_tensor(soft[m][:], b_ps[m][:], 0.0, tail[m][:], ALU.max, ALU.add)
@@ -146,46 +147,44 @@ def tile_attend_heldback_pl_kernel(tc, query, query2, keys_words, keys_scales, s
         for m in range(QT):
             nc.vector.tensor_reduce(low[m][:], neg_s[m][:], AXIS.X, ALU.min)
 
-        vt12 = sb.tile([P, 2 * P, PACK], BF16, name="vt12", tag="decay1", align_bytes=64)
-        interleave(nc.scalar.copy, vt12[:, 0:P, :], vt_ps1)
+        vt1 = sb.tile([P, P, PACK], BF16, name="vt1", tag="decay1", align_bytes=64)
+        interleave(nc.scalar.copy, vt1[:], vt_ps1)
 
         prob = [sb.tile([P, I], F32, name="prob%d" % m, align_bytes=64) for m in range(QT)]
-        z = sb.tile([P, QT], F32, name="z")
+        z = sb.tile([P, QT], F32, name="z", align_bytes=64)
         for m in range(QT):
             nc.scalar.activation(prob[m][:], neg_s[m][:], ACT.Exp, bias=low[m][:], scale=-1.0, accum_out=z[:, m : m + 1])
 
         vt_ps2 = gather_values(2, "soft1", "b_ps0")
+        vt2 = sb.tile([P, P, PACK], BF16, name="vt2", tag="neg_s1", align_bytes=64)
+        interleave(nc.scalar.copy, vt2[:], vt_ps2)
+
         rz = sb.tile([P, QT], F32, name="rz")
         nc.vector.reciprocal(rz[:], z[:])
-        w = [sb.tile([P, I], BF16, name="w%d" % m) for m in range(QT)]
-        wt_ps = [ps.tile([P, 2, P], F32, name="wt_ps%d" % m, tag=("wt0", "vt1")[m]) for m in range(QT)]
-        po = sb.tile([P, I], F32, name="po", align_bytes=64)
-        nc.gpsimd.tensor_tensor(po[:], prob[0][:], os_row[:], ALU.mult)
-        nc.scalar.activation(w[0][:].rearrange("p (u c v) -> p u c v", u=2, v=2),
-                             po[:].rearrange("p (c u v) -> p u c v", u=2, v=2), ACT.Copy, scale=rz[:, 0:1])
-        for u in range(2):
-            nc.tensor.transpose(wt_ps[0][:, u, :], w[0][:].bitcast(F32)[:, u * P : (u + 1) * P], ident[:])
-        nc.vector.scalar_tensor_tensor(
-            w[1][:].rearrange("p (n c) -> p n c", c=PACK), prob[1][:].rearrange("p (n c) -> p n c", c=PACK),
-            rz[:, 1:2], os_ps[:].rearrange("p c n -> p n c"), ALU.mult, ALU.mult)
-        turn(wt_ps[1], w[1][:])
-        vt_ps3 = gather_values(3, "prob1", "b_ps1")
-        interleave(nc.scalar.copy, vt12[:, P : 2 * P, :], vt_ps2)
+        v_ops.append(quantize("v1", vt1[:], after="z"))
         wt = sb.tile([P, Q, PACK], BF16, name="wt", align_bytes=64)
         for m in range(QT):
-            interleave(nc.scalar.copy, wt[:, m * P : (m + 1) * P, :], wt_ps[m])
+            w = sb.tile([P, I], BF16, name="w%d" % m)
+            nc.vector.scalar_tensor_tensor(
+                w[:].rearrange("p (n c) -> p n c", c=PACK), prob[m][:].rearrange("p (n c) -> p n c", c=PACK),
+                rz[:, m : m + 1], os_ps[:].rearrange("p c n -> p n c"), ALU.mult, ALU.mult)
+            wt_ps = ps.tile([P, 2, P], F32, name="wt_ps%d" % m, tag=("wt0", "vt1")[m])
+            turn(wt_ps, w[:])
+            interleave(nc.scalar.copy, wt[:, m * P : (m + 1) * P, :], wt_ps)
+
+        vt_ps3 = gather_values(3, "prob1", "b_ps1")
         w_codes, w_scales = quantize("w", wt[:], after="val_pool3")
-        codes12, scales12 = quantize("v12", vt12[:], after="wt")
+        v_ops.append(quantize("v2", vt2[:], after="wt"))
         vt3 = sb.tile([P, P, PACK], BF16, name="vt3", align_bytes=64)
         interleave(nc.scalar.copy, vt3[:], vt_ps3)
-        codes3, scales3 = quantize("v3", vt3[:], after="decay1")
-        stationary = [(v_ops[0][0][:], v_ops[0][1][:]), (codes12[:, 0:P], scales12[:, 0:P]),
-                      (codes12[:, P : 2 * P], scales12[:, P : 2 * P]), (codes3[:], scales3[:])]
+        v_ops.append(quantize("v3", vt3[:], after="neg_s1"))
 
         def product(bank, t, cols):
-            nc.tensor.matmul_mx(bank, lhsT=stationary[t][0].bitcast(FP8X4), lhsT_scale=stationary[t][1],
+            codes, scales = v_ops[t]
+            nc.tensor.matmul_mx(bank, lhsT=codes[:].bitcast(FP8X4), lhsT_scale=scales[:],
                                 rhs=w_codes[:, cols].bitcast(FP8X4), rhs_scale=w_scales[:, cols], start=True, stop=True)
 
+        last = PACK - 1
         out_rows = out_0.rearrange("(p t) q -> p t q", t=PACK)
         out_words = out_1[0].rearrange("l c r -> l (c r)").bitcast(I32)
         y = sb.tile([P, PACK, Q], F32, name="y")
@@ -193,23 +192,25 @@ def tile_attend_heldback_pl_kernel(tc, query, query2, keys_words, keys_scales, s
             bank = ps.tile([P, Q], F32, name="o_ps%d" % t, tag=tag)
             product(bank[:], t, slice(0, Q))
             nc.scalar.copy(y[:, t, :], bank[:])
-        nc.sync.dma_start(out_rows[:, 0:3, :], y[:, 0:3, :])
+        nc.sync.dma_start(out_rows[:, 0:last, :], y[:, 0:last, :])
+
         y_codes = sb.tile([P, Q], U32, name="y_codes", align_bytes=64)
         y_scales = sb.tile([P, Q], U8, name="y_scales", align_bytes=64)
         yg = []
         for m, tag in enumerate(("wt0", "vt1")):
             cols = slice(m * P, (m + 1) * P)
             bank = ps.tile([P, P], F32, name="o_ps3%d" % m, tag=tag)
-            product(bank[:], 3, cols)
-            nc.scalar.copy(y[:, 3, cols], bank[:])
+            product(bank[:], last, cols)
+            nc.scalar.copy(y[:, last, cols], bank[:])
             yg.append(sb.tile([P, P, PACK], BF16, name="yg%d" % m, align_bytes=64))
             nc.vector.tensor_copy(*grouped_views(yg[m][:], y[:, :, cols]))
-        nc.sync.dma_start(out_rows[:, 3, :], y[:, 3, :])
+        nc.sync.dma_start(out_rows[:, last, :], y[:, last, :])
         for m in range(QT):
             cols = slice(m * P, (m + 1) * P)
             nc.vector.quantize_mx(y_codes[:, cols].bitcast(FP8X4), y_scales[:, cols], yg[m][:].rearrange("p q t -> p (q t)"))
+
         nc.sync.dma_start(out_words, y_codes[:].bitcast(I32))
-        out_scales = out_2[0].bitcast(I32).rearrange("(g r) n -> r g n", r=4)
-        for r in range(4):
+        out_scales = out_2[0].bitcast(I32).rearrange("(g r) n -> r g n", r=SCALE_ROWS)
+        for r in range(SCALE_ROWS):
             queue = nc.sync if r % 2 else nc.scalar
-            queue.dma_start(out_scales[r], y_scales[:].bitcast(I32)[r:P:32, :])
+            queue.dma_start(out_scales[r], y_scales[:].bitcast(I32)[r:P:QUADRANT, :])

from contextlib import ExitStack

import concourse.mybir as mybir
from concourse.masks import make_identity

D, E, T, I, Q = 512, 512, 2048, 512, 256
FLOPS = 2 * (2 * D * Q * I + I * E * Q)

F32 = mybir.dt.float32
BF16 = mybir.dt.bfloat16
I32 = mybir.dt.int32
U32 = mybir.dt.uint32
U16 = mybir.dt.uint16
U8 = mybir.dt.uint8
FP8X4 = mybir.dt.float8_e4m3fn_x4
FP4X4 = mybir.dt.float4_e2m1fn_x4
ALU = mybir.AluOpType
ACT = mybir.ActivationFunctionType
AXIS = mybir.AxisListType

P = 128
PACK = 4
QT = Q // P
QUADRANT = 32
SCALE_ROWS = 4


def tile_attend_heldback_pl_kernel(tc, query, query2, keys_words, keys_scales, strict, slot_factor, vals, offs, out_0, out_1, out_2):
    nc = tc.nc
    with ExitStack() as ctx:
        sb = ctx.enter_context(tc.tile_pool(name="sb", bufs=1))
        ps = ctx.enter_context(tc.psum_pool(name="ps", bufs=1))

        offsets = sb.tile([P, I // 16], U16, name="offsets")
        nc.sync.dma_start(offsets[:], offs)

        os_sb = sb.tile([P, PACK], F32, name="os_sb")
        nc.sync.dma_start(os_sb[:], slot_factor.rearrange("o (p c) -> p (o c)", c=PACK))

        key_pool = sb.tile([P, T], U16, name="key_pool", align_bytes=64)
        scale_pool = sb.tile([P, T], U8, name="scale_pool", align_bytes=64)
        nc.gpsimd.memset(scale_pool[:].bitcast(I32), 0)
        nc.sync.dma_start(key_pool[:].bitcast(I32), keys_words[0].bitcast(I32))
        scale_rows = keys_scales[0].bitcast(I32).rearrange("(g r) n -> r g n", r=SCALE_ROWS)
        for r in range(SCALE_ROWS):
            nc.sync.dma_start(scale_pool[:].bitcast(I32)[r:P:QUADRANT, :], scale_rows[r])

        q2_raw = sb.tile([P, PACK, Q], F32, name="q2_raw", align_bytes=64)
        nc.sync.dma_start(q2_raw[:], query2.rearrange("(p t) q -> p t q", t=PACK))
        val_rows = vals.rearrange("(p t) n -> t p n", t=PACK)
        val_pool = [sb.tile([P, T], F32, name="val_pool%d" % t, align_bytes=64) for t in range(PACK)]
        nc.sync.dma_start(val_pool[0][:], val_rows[0])
        q_raw = sb.tile([P, PACK, Q], F32, name="q_raw")
        nc.sync.dma_start(q_raw[:], query.rearrange("(p t) q -> p t q", t=PACK))
        nc.sync.dma_start(val_pool[1][:], val_rows[1])
        strict_sb = sb.tile([P, QT], F32, name="strict_sb")
        with nc.allow_non_contiguous_dma(reason="one strictness a partition and query tile"):
            nc.sync.dma_start(strict_sb[:], strict.rearrange("(m p) o -> p (m o)", p=P))
        for t in (2, 3):
            nc.sync.dma_start(val_pool[t][:], val_rows[t])
        ident = sb.tile([P, P], F32, name="ident")
        make_identity(nc, ident[:])

        os_ps = ps.tile([P, PACK, P], F32, name="os_ps")
        for c in range(PACK):
            nc.tensor.transpose(os_ps[:, c, :], os_sb[:, c : c + 1].to_broadcast([P, P]), ident[:])

        key_g = sb.tile([P, I], U16, name="key_g", align_bytes=64)
        scale_g = sb.tile([P, I], U8, name="scale_g", align_bytes=64)
        nc.vector.tensor_copy(key_g[:], key_pool[:].indirect(offsets[:]))
        nc.vector.tensor_copy(scale_g[:], scale_pool[:].indirect(offsets[:]))

        def grouped_views(grouped, raw):
            return (
                grouped.rearrange("p (c i) t -> p c t i", i=4),
                raw.rearrange("p t (c i) -> p c t i", i=4),
            )

        def quantize(name, grouped, after=None):
            width = grouped.shape[1]
            codes = sb.tile([P, width], U32, name=name + "_codes", tag=after or name + "_codes", align_bytes=64)
            scales = sb.tile([P, width], U8, name=name + "_scales", align_bytes=64)
            nc.vector.quantize_mx(codes[:].bitcast(FP8X4), scales[:], grouped.rearrange("p c t -> p (c t)"))
            return codes, scales

        def scores(bank, codes, scales):
            nc.tensor.matmul_mx(bank, lhsT=codes.bitcast(FP8X4), lhsT_scale=scales,
                                rhs=key_g[:].bitcast(FP4X4), rhs_scale=scale_g[:], start=True, stop=True)

        b_ps = []
        q2_g = sb.tile([P, Q, PACK], BF16, name="q2_g", align_bytes=64)
        for m in range(QT):
            cols = slice(m * P, (m + 1) * P)
            nc.scalar.copy(*grouped_views(q2_g[:, cols, :], q2_raw[:, :, cols]))
            codes, scales = quantize("q2_%d" % m, q2_g[:, cols, :])
            bank = ps.tile([P, I], F32, name="b_ps%d" % m)
            scores(bank[:], codes[:], scales[:])
            b_ps.append(bank)

        mag = [sb.tile([P, I], F32, name="mag%d" % m) for m in range(QT)]
        decay = [sb.tile([P, I], F32, name="decay%d" % m, align_bytes=64) for m in range(QT)]
        tail = [sb.tile([P, I], F32, name="tail%d" % m, tag=("mag1", "tail1")[m]) for m in range(QT)]
        for m in range(QT):
            nc.scalar.activation(mag[m][:], b_ps[m][:], ACT.Abs)
            nc.scalar.activation(decay[m][:], mag[m][:], ACT.Exp, scale=-1.0)
        for m in range(QT):
            nc.scalar.activation(tail[m][:], decay[m][:], ACT.Ln, bias=1.0)

        def turn(bank, rows):
            words = rows.bitcast(F32)
            for u in range(2):
                nc.tensor.transpose(bank[:, u, :], words[:, u : 2 * P : 2], ident[:])

        def gather_values(t, after, bank_tag):
            g = sb.tile([P, I], BF16, name="val_g%d" % t, tag=after, align_bytes=64)
            nc.vector.tensor_copy(g[:], val_pool[t][:].indirect(offsets[:]))
            bank = ps.tile([P, 2, P], F32, name="vt_ps%d" % t, tag=bank_tag)
            turn(bank, g[:])
            return bank

        def interleave(copy, grouped, bank):
            copy(grouped.bitcast(F32), bank[:].rearrange("p u c -> p c u"))

        vt_ps0 = gather_values(0, "q2_raw", "vt0")

        q_g = sb.tile([P, Q, PACK], BF16, name="q_g", tag="val_pool0", align_bytes=64)
        nc.vector.tensor_copy(*grouped_views(q_g[:], q_raw[:]))
        vt0 = sb.tile([P, P, PACK], BF16, name="vt0", align_bytes=64)
        interleave(nc.vector.tensor_copy, vt0[:], vt_ps0)
        q_codes, q_scales = quantize("q", q_g[:])
        v_ops = [quantize("v0", vt0[:])]
        vt_ps1 = gather_values(1, "val_pool0", "vt1")
        a_ps = []
        for m in range(QT):
            cols = slice(m * P, (m + 1) * P)
            bank = ps.tile([P, I], F32, name="a_ps%d" % m)
            scores(bank[:], q_codes[:, cols], q_scales[:, cols])
            a_ps.append(bank)

        soft = [sb.tile([P, I], F32, name="soft%d" % m, tag=("val_pool1", "soft1")[m], align_bytes=64) for m in range(QT)]
        neg_s = [sb.tile([P, I], F32, name="neg_s%d" % m, align_bytes=64) for m in range(QT)]
        low = [sb.tile([P, 1], F32, name="low%d" % m) for m in range(QT)]
        for m in range(QT):
            nc.vector.scalar_tensor_tensor(soft[m][:], b_ps[m][:], 0.0, tail[m][:], ALU.max, ALU.add)
        for m in range(QT):
            nc.vector.scalar_tensor_tensor(neg_s[m][:], soft[m][:], strict_sb[:, m : m + 1], a_ps[m][:], ALU.mult, ALU.subtract)
        for m in range(QT):
            nc.vector.tensor_reduce(low[m][:], neg_s[m][:], AXIS.X, ALU.min)

        vt1 = sb.tile([P, P, PACK], BF16, name="vt1", tag="decay1", align_bytes=64)
        interleave(nc.scalar.copy, vt1[:], vt_ps1)

        prob = [sb.tile([P, I], F32, name="prob%d" % m, align_bytes=64) for m in range(QT)]
        z = sb.tile([P, QT], F32, name="z", align_bytes=64)
        for m in range(QT):
            nc.scalar.activation(prob[m][:], neg_s[m][:], ACT.Exp, bias=low[m][:], scale=-1.0, accum_out=z[:, m : m + 1])

        vt_ps2 = gather_values(2, "soft1", "b_ps0")
        vt2 = sb.tile([P, P, PACK], BF16, name="vt2", tag="neg_s1", align_bytes=64)
        interleave(nc.scalar.copy, vt2[:], vt_ps2)

        rz = sb.tile([P, QT], F32, name="rz")
        nc.vector.reciprocal(rz[:], z[:])
        v_ops.append(quantize("v1", vt1[:], after="z"))
        wt = sb.tile([P, Q, PACK], BF16, name="wt", align_bytes=64)
        for m in range(QT):
            w = sb.tile([P, I], BF16, name="w%d" % m)
            nc.vector.scalar_tensor_tensor(
                w[:].rearrange("p (n c) -> p n c", c=PACK), prob[m][:].rearrange("p (n c) -> p n c", c=PACK),
                rz[:, m : m + 1], os_ps[:].rearrange("p c n -> p n c"), ALU.mult, ALU.mult)
            wt_ps = ps.tile([P, 2, P], F32, name="wt_ps%d" % m, tag=("wt0", "vt1")[m])
            turn(wt_ps, w[:])
            interleave(nc.scalar.copy, wt[:, m * P : (m + 1) * P, :], wt_ps)

        vt_ps3 = gather_values(3, "prob1", "b_ps1")
        w_codes, w_scales = quantize("w", wt[:], after="val_pool3")
        v_ops.append(quantize("v2", vt2[:], after="wt"))
        vt3 = sb.tile([P, P, PACK], BF16, name="vt3", align_bytes=64)
        interleave(nc.scalar.copy, vt3[:], vt_ps3)
        v_ops.append(quantize("v3", vt3[:], after="neg_s1"))

        def product(bank, t, cols):
            codes, scales = v_ops[t]
            nc.tensor.matmul_mx(bank, lhsT=codes[:].bitcast(FP8X4), lhsT_scale=scales[:],
                                rhs=w_codes[:, cols].bitcast(FP8X4), rhs_scale=w_scales[:, cols], start=True, stop=True)

        last = PACK - 1
        out_rows = out_0.rearrange("(p t) q -> p t q", t=PACK)
        out_words = out_1[0].rearrange("l c r -> l (c r)").bitcast(I32)
        y = sb.tile([P, PACK, Q], F32, name="y")
        for t, tag in enumerate(("a_ps0", "a_ps1", "vt0")):
            bank = ps.tile([P, Q], F32, name="o_ps%d" % t, tag=tag)
            product(bank[:], t, slice(0, Q))
            nc.scalar.copy(y[:, t, :], bank[:])
        nc.sync.dma_start(out_rows[:, 0:last, :], y[:, 0:last, :])

        y_codes = sb.tile([P, Q], U32, name="y_codes", align_bytes=64)
        y_scales = sb.tile([P, Q], U8, name="y_scales", align_bytes=64)
        yg = []
        for m, tag in enumerate(("wt0", "vt1")):
            cols = slice(m * P, (m + 1) * P)
            bank = ps.tile([P, P], F32, name="o_ps3%d" % m, tag=tag)
            product(bank[:], last, cols)
            nc.scalar.copy(y[:, last, cols], bank[:])
            yg.append(sb.tile([P, P, PACK], BF16, name="yg%d" % m, align_bytes=64))
            nc.vector.tensor_copy(*grouped_views(yg[m][:], y[:, :, cols]))
        nc.sync.dma_start(out_rows[:, last, :], y[:, last, :])
        for m in range(QT):
            cols = slice(m * P, (m + 1) * P)
            nc.vector.quantize_mx(y_codes[:, cols].bitcast(FP8X4), y_scales[:, cols], yg[m][:].rearrange("p q t -> p (q t)"))

        nc.sync.dma_start(out_words, y_codes[:].bitcast(I32))
        out_scales = out_2[0].bitcast(I32).rearrange("(g r) n -> r g n", r=SCALE_ROWS)
        for r in range(SCALE_ROWS):
            queue = nc.sync if r % 2 else nc.scalar
            queue.dma_start(out_scales[r], y_scales[:].bitcast(I32)[r:P:QUADRANT, :])
